import numpy as np
import ml_dtypes


def mxq(x, axis, fmt="e4m3"):
    dtype, down = {"e4m3": (ml_dtypes.float8_e4m3fn, 7), "e5m2": (ml_dtypes.float8_e5m2, 14)}[fmt]
    v = np.moveaxis(np.asarray(x, np.float32).astype(ml_dtypes.bfloat16).astype(np.float64), axis, -1)
    blocks = v.reshape(v.shape[:-1] + (-1, 32))
    amax = np.abs(blocks).max(-1, keepdims=True)
    byte = np.maximum(np.where(amax > 0, np.frexp(amax)[1] - 1 + 127, 0) - down, 1)
    scale = np.exp2(byte - 127.0)
    codes = (blocks / scale).astype(np.float32).astype(dtype).astype(np.float64)
    return np.moveaxis((codes * scale).reshape(v.shape), -1, axis)


WIDE = False


def mx_kscale(k):
    if not WIDE:
        return np.ones(k)
    levels = np.array([10, -10, 5, -5, 0])
    if k % 512:
        return np.exp2(np.random.permutation(np.resize(levels, k // 32))).repeat(32)
    a = np.empty((k // 512, 16))
    for p in range(k // 512):
        a[p, :8] = np.random.permutation(np.resize(levels, 8))
        for g in range(8):
            far = levels[np.abs(levels - a[p, g]) >= 10]
            a[p, g + 8] = far[np.random.randint(len(far))]
    return np.exp2(a.ravel()).repeat(32)


def f64(x):
    return np.asarray(x).astype(np.float64)


def striped(idx):
    return np.tile(idx.reshape(-1, 16).T, (8, 1)).astype(np.uint16)


def unstriped(offs):
    return offs[:16].T.reshape(-1).astype(np.int64)


def striped8(idx):
    return np.concatenate([x.reshape(-1, 16).T for x in idx]).astype(np.uint16)


def runs(offs, k):
    lists = np.stack([offs[16 * r : 16 * r + 16].T.reshape(-1) for r in range(8)]).astype(np.int64)
    return lists[np.arange(k) % 512 // 64]


def pack_weight(w):
    k, n = w.shape
    w = f64(np.asarray(w, np.float32).astype(ml_dtypes.bfloat16)).reshape(k // 32, 32, n)
    amax = np.abs(w).max(1)
    byte = np.clip(np.where(amax > 0, np.frexp(amax)[1] - 1 + 127 - 7, 1), 1, 254)
    scaled = (w * np.exp2(127.0 - byte)[:, None, :]).reshape(k, n).astype(np.float32)
    words = np.ascontiguousarray(scaled.reshape(k // 512, 128, 4, n).transpose(0, 1, 3, 2)).astype(ml_dtypes.float8_e4m3fn).view(np.uint8)
    return words, np.ascontiguousarray(byte.astype(np.uint8).reshape(k // 512, 16, n))


def unpack_weight(words, scales):
    g, p, n, _ = words.shape
    vals = np.ascontiguousarray(words).view(ml_dtypes.float8_e4m3fn).astype(np.float64) * np.repeat(np.exp2(scales.astype(np.float64) - 127.0), 8, axis=1)[..., None]
    return vals.transpose(0, 1, 3, 2).reshape(g * 512, n)

def planes(y):
    n, m = y.shape
    v = y.astype(np.float32).astype(ml_dtypes.bfloat16).astype(np.float64).reshape(n // 32, 32, m)
    top = np.abs(v).max(1)
    byte = np.clip(np.where(top > 0, np.frexp(top)[1] - 1 + 127 - 7, 1), 1, 254)
    codes = (v * np.exp2(127.0 - byte)[:, None, :]).reshape(n, m).astype(np.float32).astype(ml_dtypes.float8_e4m3fn).view(np.uint8)
    words = codes.reshape(n // 512, 128, 4, m).transpose(0, 1, 3, 2)
    return np.ascontiguousarray(words), np.ascontiguousarray(byte.astype(np.uint8).reshape(n // 512, 16, m))


K, T, S, N, H, J = 512, 2048, 512, 512, 512, 512


def setup_inputs():
    n = np.random.standard_normal
    s = mx_kscale(K)[:, None]
    u = mx_kscale(S)
    packed_xT = pack_weight(n((K, T)) * s)
    return {
        "x_words": packed_xT[0],
        "x_scales": packed_xT[1],
        "wa": (n((K, H)) / np.sqrt(K) / s).astype(np.float32),
        "wb": (n((K, N)) / np.sqrt(K) / s).astype(np.float32),
        "tab": n((S, J)).astype(np.float32),
        "gt": (np.random.uniform(0.5, 1.5, (S, 1)) * u[:, None]).astype(np.float32),
        "gi": (np.random.uniform(0.5, 1.5, (S, 1)) / u[:, None]).astype(np.float32),
        "offs": striped(np.random.permutation(T)[:S]),
        "two": striped(np.random.permutation(T)[:S]),
        "n1": striped8(np.random.randint(0, J, (8, H))),
        "n2": striped8(np.random.randint(0, J, (8, H))),
        "n3": striped8(np.stack([np.random.permutation(H) for _ in range(8)])),
        "n4": striped8(np.stack([np.random.permutation(N) for _ in range(8)])),
        "n5": striped8(np.stack([np.random.permutation(N) for _ in range(8)])),
        "n6": striped8(np.stack([np.random.permutation(N) for _ in range(8)])),
        "n7": striped8(np.stack([np.random.permutation(N) for _ in range(8)])),
    }


def reference(x_words, x_scales, wa, wb, tab, gt, gi, offs, two, n1, n2, n3, n4, n5, n6, n7):
    xq = unpack_weight(x_words, x_scales)[:, unstriped(offs)]
    a = xq.T @ mxq(f64(wa), 0, "e4m3")
    z = f64(gt) * ((a[np.arange(S)[:, None], runs(n3, S)]) * (f64(tab)[np.arange(S)[:, None], runs(n1, S)]) + f64(tab)[np.arange(S)[:, None], runs(n2, S)])
    x_two = unpack_weight(x_words, x_scales)[:, unstriped(two)]
    b = x_two.T @ mxq(f64(wb), 0, "e4m3")
    z2 = f64(gi) * ((np.tanh(b[np.arange(S)[:, None], runs(n4, S)] - b)) * (b[np.arange(S)[:, None], runs(n5, S)]))
    cv = 0.0625 * ((mxq(z, 0, "e4m3").T @ mxq(z2, 0, "e4m3")))
    out_0 = 0.75 * (cv[np.arange(H)[:, None], runs(n6, H)] + cv[np.arange(H)[:, None], runs(n7, H)]) - cv
    return (out_0,) + planes(out_0)

@@ -1,0 +1,252 @@
+from contextlib import ExitStack
+
+import concourse.mybir as mybir
+
+K, T, S, N, H, J = 512, 2048, 512, 512, 512, 512
+FLOPS = 2 * K * S * H + 2 * K * S * N + 2 * S * H * N
+
+F32 = mybir.dt.float32
+BF16 = mybir.dt.bfloat16
+I32 = mybir.dt.int32
+U32 = mybir.dt.uint32
+U16 = mybir.dt.uint16
+U8 = mybir.dt.uint8
+FP8X4 = mybir.dt.float8_e4m3fn_x4
+ALU = mybir.AluOpType
+ACT = mybir.ActivationFunctionType
+
+P = 128
+PACK = 4
+WIDE = 2 * 512
+HALF = 256
+QUARTER = 128
+
+
+def tile_picked_mombkindafdiflap_none_po_kernel(
+    tc, x_words, x_scales, wa, wb, tab, gt, gi, offs, two, n1, n2, n3, n4, n5, n6, n7, out_0, out_1, out_2
+):
+    nc = tc.nc
+
+    with ExitStack() as ctx:
+        lists = ctx.enter_context(tc.tile_pool(name="lists", bufs=1))
+        keep = ctx.enter_context(tc.tile_pool(name="keep", bufs=1))
+        psum = ctx.enter_context(tc.psum_pool(name="psum", bufs=8))
+
+        def load_list(name, src):
+            held = lists.tile([P, S // 16], U16, name=name)
+            nc.sync.dma_start(held[:], src)
+            return held
+
+        def entries(held, lo, hi):
+            return held[:, lo // 16 : hi // 16]
+
+        def tiles(name, shape, dtype):
+            return [keep.tile(shape, dtype, name="%s%d" % (name, t), tag="%s%d" % (name, t), align_bytes=64) for t in range(PACK)]
+
+        def mx_operand(name, width):
+            rounded = keep.tile([P, width, PACK], BF16, name=name + "_bf16", tag=name + "_bf16", align_bytes=64)
+            codes = keep.tile([P, width], U32, name=name + "_codes", align_bytes=64)
+            scales = keep.tile([P, width], U8, name=name + "_scales", align_bytes=64)
+            return rounded, codes, scales
+
+        def quantize(rounded, codes, scales):
+            nc.vector.quantize_mx(out=codes.bitcast(FP8X4), scales=scales, in_=rounded.rearrange("p c t -> p (c t)"))
+
+        def interleave(copy, rounded, rows):
+            copy(
+                out=rounded.rearrange("p (c i) t -> p c t i", i=PACK),
+                in_=rows.rearrange("p t (c i) -> p c t i", i=PACK),
+            )
+
+        def product(lhs_codes, lhs_scales, t, rhs_codes, rhs_scales):
+            bank = psum.tile([P, 512], F32, name="bank")
+            acc = bank[:, 0 : rhs_codes.shape[1]]
+            cols = slice(t * P, (t + 1) * P)
+            nc.tensor.matmul_mx(
+                out=acc,
+                lhsT=lhs_codes[:, cols].bitcast(FP8X4),
+                lhsT_scale=lhs_scales[:, cols],
+                rhs=rhs_codes.bitcast(FP8X4),
+                rhs_scale=rhs_scales,
+                start=True,
+                stop=True,
+            )
+            return acc
+
+        warm_in = keep.tile([P, 1], F32, name="warm_in")
+        warm_out = keep.tile([P, 1], F32, name="warm_out")
+        nc.gpsimd.memset(warm_in[:], 0.0)
+        nc.scalar.activation(out=warm_out[:], in_=warm_in[:], func=ACT.Tanh)
+
+        xs = keep.tile([P, T], U8, name="xs")
+        nc.vector.memset(xs[:].bitcast(I32), 0)
+
+        gt_sb = keep.tile([P, PACK], F32, name="gt_sb")
+        gi_sb = keep.tile([P, PACK], F32, name="gi_sb")
+        nc.scalar.dma_start(gt_sb[:], gt.rearrange("(p t) o -> p (t o)", t=PACK))
+        nc.scalar.dma_start(gi_sb[:], gi.rearrange("(p t) o -> p (t o)", t=PACK))
+
+        tab_rows = tab.rearrange("(p t) c -> p t c", t=PACK)
+        tab_win = tiles("tab_win", [P, WIDE], F32)
+        xw = keep.tile([P, T], U32, name="xw")
+        wa_raw = keep.tile([P, PACK, H], F32, name="wa_raw")
+        wb_raw = keep.tile([P, PACK, N], F32, name="wb_raw")
+
+        n1_sb = load_list("n1_sb", n1)
+        for t in range(PACK - 1):
+            nc.sync.dma_start(tab_win[t][:, 0:J], tab_rows[:, t, :])
+        nc.sync.dma_start(xw[:].bitcast(I32), x_words[0].rearrange("p c r -> p (c r)").bitcast(I32))
+        offs_sb = load_list("offs_sb", offs)
+        two_sb = load_list("two_sb", two)
+        for q in range(4):
+            nc.sync.dma_start(xs[32 * q : 32 * q + 4, :].bitcast(I32), x_scales[0][4 * q : 4 * q + 4, :].bitcast(I32))
+        nc.sync.dma_start(wa_raw[:], wa.rearrange("(p j) c -> p j c", j=PACK))
+        nc.sync.dma_start(tab_win[PACK - 1][:, 0:J], tab_rows[:, PACK - 1, :])
+        n3_sb = load_list("n3_sb", n3)
+        n2_sb = load_list("n2_sb", n2)
+        nc.sync.dma_start(wb_raw[:], wb.rearrange("(p j) c -> p j c", j=PACK))
+        n4_sb = load_list("n4_sb", n4)
+        n5_sb = load_list("n5_sb", n5)
+        n6_sb = load_list("n6_sb", n6)
+        n7_sb = load_list("n7_sb", n7)
+
+        tab_n1 = []
+
+        def fetch_tab_n1(t, tag):
+            tab_n1.append(keep.tile([P, H], F32, name="tab_n1_%d" % t, tag=tag, align_bytes=64))
+            nc.vector.tensor_copy(tab_n1[t][:], tab_win[t][:].indirect(n1_sb[:]))
+            nc.scalar.activation(out=tab_win[t][:, 0:J], in_=tab_win[t][:, 0:J], func=ACT.Copy, scale=gt_sb[:, t : t + 1])
+
+        def pick(name, held):
+            words = keep.tile([P, S], U32, name=name + "_words", align_bytes=64)
+            picked = keep.tile([P, S], U8, name=name + "_picked", align_bytes=64)
+            dealt = keep.tile([P, S], U8, name=name + "_dealt", align_bytes=64)
+            nc.vector.tensor_copy(words[:].rearrange("p (t m) -> p m t", t=PACK), xw[:].indirect(held[:]))
+            nc.vector.tensor_copy(picked[:], xs[:].indirect(held[:]))
+            nc.vector.tensor_copy(
+                dealt[:].rearrange("p (t m) -> p m t", t=PACK), picked[:].rearrange("p (m t) -> p m t", t=PACK)
+            )
+            return words, dealt
+
+        for t in range(PACK - 1):
+            fetch_tab_n1(t, "tab_n1_%d" % t)
+        xa_words, xa_scales = pick("xa", offs_sb)
+        xb_words, xb_scales = pick("xb", two_sb)
+
+        wa_bf, wa_codes, wa_scales = mx_operand("wa", H)
+        interleave(nc.scalar.copy, wa_bf[:], wa_raw[:])
+        quantize(wa_bf[:], wa_codes[:], wa_scales[:])
+        fetch_tab_n1(PACK - 1, "wa_bf16")
+
+        a_win = tiles("a_win", [P, WIDE], F32)
+        for t in range(PACK):
+            acc = product(xa_words, xa_scales, t, wa_codes[:], wa_scales[:])
+            nc.scalar.activation(out=a_win[t][:, 0:H], in_=acc, func=ACT.Copy, scale=gt_sb[:, t : t + 1])
+
+        wb_bf, wb_codes, wb_scales = mx_operand("wb", N)
+        for lo in (0, HALF):
+            interleave(nc.scalar.copy, wb_bf[:, lo : lo + HALF, :], wb_raw[:, :, lo : lo + HALF])
+
+        a_tab = tiles("a_tab", [P, H], F32)
+        for t in range(PACK):
+            nc.vector.tensor_tensor(a_tab[t][:], a_win[t][:].indirect(n3_sb[:]), tab_n1[t][:], ALU.mult)
+        quantize(wb_bf[:], wb_codes[:], wb_scales[:])
+
+        b_win = tiles("b_win", [P, WIDE], F32)
+        b_plain = tiles("b_plain", [P, N], F32)
+        gb_win = tiles("gb_win", [P, N], F32)
+        b_acc = []
+        for t in range(PACK):
+            acc = product(xb_words, xb_scales, t, wb_codes[:], wb_scales[:])
+            nc.scalar.copy(out=b_win[t][:, 0:N], in_=acc)
+            nc.sync.dma_start(b_plain[t][:], b_win[t][:, 0:N])
+            b_acc.append(acc)
+        for t in range(PACK):
+            nc.scalar.activation(out=gb_win[t][:], in_=b_acc[t], func=ACT.Copy, scale=gi_sb[:, t : t + 1])
+
+        z = keep.tile([P, PACK, H], F32, name="z", tag="wb_bf16", align_bytes=64)
+        for t in range(PACK):
+            nc.vector.tensor_tensor(z[:, t, :], tab_win[t][:].indirect(n2_sb[:]), a_tab[t][:], ALU.add)
+
+        z_bf, z_codes, z_scales = mx_operand("z", H)
+        nc.scalar.copy(
+            out=z_bf[:].rearrange("p (h m) t -> p m h t", h=PACK),
+            in_=z[:].rearrange("p t (m h) -> p m h t", h=PACK),
+        )
+
+        diff = tiles("diff", [P, N], F32)
+        tanh_halves = (tiles("tanh_low", [P, HALF], F32), tiles("tanh_high", [P, HALF], F32))
+        for t in range(PACK):
+            nc.vector.tensor_tensor(diff[t][:], b_win[t][:].indirect(n4_sb[:]), b_plain[t][:], ALU.subtract)
+            for h in range(2):
+                nc.scalar.activation(out=tanh_halves[h][t][:], in_=diff[t][:, h * HALF : (h + 1) * HALF], func=ACT.Tanh)
+        quantize(z_bf[:], z_codes[:], z_scales[:])
+
+        cv_win = tiles("cv_win", [P, WIDE], F32)
+        cv_plain = tiles("cv_plain", [P, N], F32)
+
+        def leave_bank(t, acc, lo, hi):
+            nc.scalar.activation(out=cv_win[t][:, lo:hi], in_=acc, func=ACT.Copy, scale=0.75 * 0.0625)
+            nc.scalar.activation(out=cv_plain[t][:, lo:hi], in_=acc, func=ACT.Copy, scale=0.0625)
+
+        z2_codes = keep.tile([P, N], U32, name="z2_codes", align_bytes=64)
+        z2_scales = keep.tile([P, N], U8, name="z2_scales", align_bytes=64)
+
+        def z2_columns(z2, lo, hi):
+            z2_bf = keep.tile([P, hi - lo, PACK], BF16, name="z2_bf16_%d" % lo, align_bytes=64)
+            for t in range(PACK):
+                tanh = tanh_halves[lo // HALF][t][:, lo % HALF : lo % HALF + hi - lo]
+                nc.vector.tensor_tensor(z2[:, t, :], gb_win[t][:].indirect(entries(n5_sb, lo, hi)), tanh, ALU.mult)
+            interleave(nc.scalar.copy if hi < N else nc.vector.tensor_copy, z2_bf[:], z2)
+            quantize(z2_bf[:], z2_codes[:, lo:hi], z2_scales[:, lo:hi])
+            leave_bank(0, product(z_codes, z_scales, 0, z2_codes[:, lo:hi], z2_scales[:, lo:hi]), lo, hi)
+
+        z2_low = keep.tile([P, PACK, HALF], F32, name="z2_low")
+        z2_columns(z2_low[:], 0, HALF)
+        z2_high = keep.tile([P, 2, PACK, QUARTER], F32, name="z2_high", tag="tanh_low3", align_bytes=64)
+        for c in range(2):
+            z2_columns(z2_high[:, c], HALF + c * QUARTER, HALF + (c + 1) * QUARTER)
+        for t in range(1, PACK):
+            leave_bank(t, product(z_codes, z_scales, t, z2_codes[:], z2_scales[:]), 0, N)
+
+        out_rows = out_0.rearrange("(p t) c -> p t c", t=PACK)
+        out_words = out_1[0].rearrange("p c r -> p (c r)").bitcast(I32)
+        out_scales = keep.tile([P, N], U8, name="out_scales", align_bytes=64)
+        part = tiles("part", [P, N], F32)
+        gate = keep.tile([P, HALF], F32, name="gate", tag="gate", align_bytes=64)
+        y_low = keep.tile([P, PACK, HALF], F32, name="y_low")
+
+        def y_rows(y, t, lo, other):
+            nc.vector.tensor_tensor(y[:, t, :], cv_win[t][:].indirect(entries(n7_sb, lo, lo + HALF)), other, ALU.add)
+            nc.sync.dma_start(out_rows[:, t, lo : lo + HALF], y[:, t, :])
+
+        def y_planes(y, lo, copies):
+            y_bf = keep.tile([P, HALF, PACK], BF16, name="y_bf16_%d" % lo, align_bytes=64)
+            y_codes = keep.tile([P, HALF], U32, name="y_codes_%d" % lo, align_bytes=64)
+            share = HALF // len(copies)
+            for c, copy in enumerate(copies):
+                interleave(copy, y_bf[:, c * share : (c + 1) * share, :], y[:, :, c * share : (c + 1) * share])
+            quantize(y_bf[:], y_codes[:], out_scales[:, lo : lo + HALF])
+            nc.sync.dma_start(out_words[:, lo : lo + HALF], y_codes[:].bitcast(I32))
+
+        last = PACK - 1
+        for t in range(last):
+            nc.vector.tensor_tensor(part[t][:], cv_win[t][:].indirect(n6_sb[:]), cv_plain[t][:], ALU.subtract)
+            y_rows(y_low, t, 0, part[t][:, 0:HALF])
+        nc.vector.tensor_tensor(
+            gate[:], cv_win[last][:].indirect(entries(n6_sb, 0, HALF)), cv_plain[last][:, 0:HALF], ALU.subtract
+        )
+        nc.vector.tensor_tensor(
+            part[last][:, HALF:N], cv_win[last][:].indirect(entries(n6_sb, HALF, N)), cv_plain[last][:, HALF:N], ALU.subtract
+        )
+        y_rows(y_low, last, 0, gate[:])
+        y_planes(y_low, 0, [nc.scalar.copy])
+        y_high = keep.tile([P, PACK, HALF], F32, name="y_high", tag="gate", align_bytes=64)
+        for t in range(PACK):
+            y_rows(y_high, t, HALF, part[t][:, HALF:N])
+        y_planes(y_high, HALF, [nc.scalar.copy, nc.vector.tensor_copy])
+        for q in range(4):
+            queue = nc.scalar if q % 2 else nc.sync
+            queue.dma_start(
+                out_2[0][4 * q : 4 * q + 4, :].bitcast(I32), out_scales[32 * q : 32 * q + 4, :].bitcast(I32)
+            )

@@ -20,6 +20,8 @@ PACK = 4
 WIDE = 2 * 512
 HALF = 256
 QUARTER = 128
+CV_SCALE = 0.0625
+WIN_SCALE = 0.75 * CV_SCALE
 
 
 def tile_picked_mombkindafdiflap_none_po_kernel(
@@ -83,74 +85,97 @@ def tile_picked_mombkindafdiflap_none_po_kernel(
 
         gt_sb = keep.tile([P, PACK], F32, name="gt_sb")
         gi_sb = keep.tile([P, PACK], F32, name="gi_sb")
-        nc.scalar.dma_start(gt_sb[:], gt.rearrange("(p t) o -> p (t o)", t=PACK))
-        nc.scalar.dma_start(gi_sb[:], gi.rearrange("(p t) o -> p (t o)", t=PACK))
 
         tab_rows = tab.rearrange("(p t) c -> p t c", t=PACK)
         tab_win = tiles("tab_win", [P, WIDE], F32)
         xw = keep.tile([P, T], U32, name="xw")
-        wa_raw = keep.tile([P, PACK, H], F32, name="wa_raw")
-        wb_raw = keep.tile([P, PACK, N], F32, name="wb_raw")
 
+        def load_weights(name, w, h):
+            raw = keep.tile([P, PACK, HALF], F32, name="%s_raw%d" % (name, h), tag="%s_raw%d" % (name, h), align_bytes=64)
+            nc.sync.dma_start(raw[:], w.rearrange("(p j) c -> p j c", j=PACK)[:, :, h * HALF : (h + 1) * HALF])
+            return raw
+
+        nc.sync.dma_start(tab_win[0][:, 0:J], tab_rows[:, 0, :])
         n1_sb = load_list("n1_sb", n1)
-        for t in range(PACK - 1):
+        for t in range(1, PACK - 1):
             nc.sync.dma_start(tab_win[t][:, 0:J], tab_rows[:, t, :])
+        nc.sync.dma_start(gt_sb[:], gt.rearrange("(p t) o -> p (t o)", t=PACK))
         nc.sync.dma_start(xw[:].bitcast(I32), x_words[0].rearrange("p c r -> p (c r)").bitcast(I32))
         offs_sb = load_list("offs_sb", offs)
         two_sb = load_list("two_sb", two)
         for q in range(4):
             nc.sync.dma_start(xs[32 * q : 32 * q + 4, :].bitcast(I32), x_scales[0][4 * q : 4 * q + 4, :].bitcast(I32))
-        nc.sync.dma_start(wa_raw[:], wa.rearrange("(p j) c -> p j c", j=PACK))
+        wa_raw = [load_weights("wa", wa, h) for h in range(2)]
+        wb_raw = [load_weights("wb", wb, 0)]
         nc.sync.dma_start(tab_win[PACK - 1][:, 0:J], tab_rows[:, PACK - 1, :])
         n3_sb = load_list("n3_sb", n3)
+        wb_raw.append(load_weights("wb", wb, 1))
         n2_sb = load_list("n2_sb", n2)
-        nc.sync.dma_start(wb_raw[:], wb.rearrange("(p j) c -> p j c", j=PACK))
+        nc.sync.dma_start(gi_sb[:], gi.rearrange("(p t) o -> p (t o)", t=PACK))
         n4_sb = load_list("n4_sb", n4)
         n5_sb = load_list("n5_sb", n5)
         n6_sb = load_list("n6_sb", n6)
         n7_sb = load_list("n7_sb", n7)
 
+        last = PACK - 1
         tab_n1 = []
 
         def fetch_tab_n1(t, tag):
             tab_n1.append(keep.tile([P, H], F32, name="tab_n1_%d" % t, tag=tag, align_bytes=64))
             nc.vector.tensor_copy(tab_n1[t][:], tab_win[t][:].indirect(n1_sb[:]))
+
+        def weigh_tab(t):
             nc.scalar.activation(out=tab_win[t][:, 0:J], in_=tab_win[t][:, 0:J], func=ACT.Copy, scale=gt_sb[:, t : t + 1])
 
         def pick(name, held):
             words = keep.tile([P, S], U32, name=name + "_words", align_bytes=64)
             picked = keep.tile([P, S], U8, name=name + "_picked", align_bytes=64)
-            dealt = keep.tile([P, S], U8, name=name + "_dealt", align_bytes=64)
             nc.vector.tensor_copy(words[:].rearrange("p (t m) -> p m t", t=PACK), xw[:].indirect(held[:]))
             nc.vector.tensor_copy(picked[:], xs[:].indirect(held[:]))
-            nc.vector.tensor_copy(
-                dealt[:].rearrange("p (t m) -> p m t", t=PACK), picked[:].rearrange("p (m t) -> p m t", t=PACK)
-            )
-            return words, dealt
+            return words, picked
 
-        for t in range(PACK - 1):
+        def deal(name, picked, tag):
+            dealt = keep.tile([P, S], U8, name=name, tag=tag, align_bytes=64)
+            nc.vector.tensor_copy(
+                dealt[:].rearrange("p (t m) -> p t m", t=PACK), picked[:].rearrange("p (m t) -> p t m", t=PACK)
+            )
+            return dealt
+
+        for t in range(last):
             fetch_tab_n1(t, "tab_n1_%d" % t)
-        xa_words, xa_scales = pick("xa", offs_sb)
-        xb_words, xb_scales = pick("xb", two_sb)
+            weigh_tab(t)
+        xa_words, xa_picked = pick("xa", offs_sb)
+        xb_words, xb_picked = pick("xb", two_sb)
+        xa_scales = deal("xa_scales", xa_picked, "xa_scales")
 
         wa_bf, wa_codes, wa_scales = mx_operand("wa", H)
-        interleave(nc.scalar.copy, wa_bf[:], wa_raw[:])
+        for h in range(2):
+            interleave(nc.scalar.copy, wa_bf[:, h * HALF : (h + 1) * HALF, :], wa_raw[h][:])
         quantize(wa_bf[:], wa_codes[:], wa_scales[:])
-        fetch_tab_n1(PACK - 1, "wa_bf16")
+        xb_scales = deal("xb_scales", xb_picked, "wa_raw1")
+        fetch_tab_n1(last, "wa_bf16")
 
         a_win = tiles("a_win", [P, WIDE], F32)
         for t in range(PACK):
-            acc = product(xa_words, xa_scales, t, wa_codes[:], wa_scales[:])
-            nc.scalar.activation(out=a_win[t][:, 0:H], in_=acc, func=ACT.Copy, scale=gt_sb[:, t : t + 1])
+            for lo, hi in ((0, HALF), (HALF, H)) if t == 0 else ((0, H),):
+                acc = product(xa_words, xa_scales, t, wa_codes[:, lo:hi], wa_scales[:, lo:hi])
+                nc.scalar.activation(out=a_win[t][:, lo:hi], in_=acc, func=ACT.Copy, scale=gt_sb[:, t : t + 1])
 
         wb_bf, wb_codes, wb_scales = mx_operand("wb", N)
-        for lo in (0, HALF):
-            interleave(nc.scalar.copy, wb_bf[:, lo : lo + HALF, :], wb_raw[:, :, lo : lo + HALF])
+        for h in range(2):
+            interleave(nc.scalar.copy, wb_bf[:, h * HALF : (h + 1) * HALF, :], wb_raw[h][:])
+        weigh_tab(last)
 
-        a_tab = tiles("a_tab", [P, H], F32)
-        for t in range(PACK):
+        a_tab = []
+
+        def fetch_a(t, tag):
+            a_tab.append(keep.tile([P, H], F32, name="a_tab%d" % t, tag=tag, align_bytes=64))
             nc.vector.tensor_tensor(a_tab[t][:], a_win[t][:].indirect(n3_sb[:]), tab_n1[t][:], ALU.mult)
+
+        for t in range(last):
+            fetch_a(t, "a_tab%d" % t)
         quantize(wb_bf[:], wb_codes[:], wb_scales[:])
+        fetch_a(last, "wb_raw1")
 
         b_win = tiles("b_win", [P, WIDE], F32)
         b_plain = tiles("b_plain", [P, N], F32)
@@ -168,26 +193,18 @@ def tile_picked_mombkindafdiflap_none_po_kernel(
         for t in range(PACK):
             nc.vector.tensor_tensor(z[:, t, :], tab_win[t][:].indirect(n2_sb[:]), a_tab[t][:], ALU.add)
 
-        z_bf, z_codes, z_scales = mx_operand("z", H)
-        nc.scalar.copy(
-            out=z_bf[:].rearrange("p (h m) t -> p m h t", h=PACK),
-            in_=z[:].rearrange("p t (m h) -> p m h t", h=PACK),
-        )
-
+        z_bf = keep.tile([P, H, PACK], BF16, name="z_bf16", align_bytes=64)
+        z_dealt = z_bf[:].rearrange("p (h m) t -> p m h t", h=PACK)
+        z_quads = z[:].rearrange("p t (m h) -> p m h t", h=PACK)
         diff = tiles("diff", [P, N], F32)
         tanh_halves = (tiles("tanh_low", [P, HALF], F32), tiles("tanh_high", [P, HALF], F32))
         for t in range(PACK):
             nc.vector.tensor_tensor(diff[t][:], b_win[t][:].indirect(n4_sb[:]), b_plain[t][:], ALU.subtract)
+            if t % 2 == 0:
+                quads = slice(t * P // PACK, (t + 2) * P // PACK)
+                nc.scalar.copy(out=z_dealt[:, quads], in_=z_quads[:, quads])
             for h in range(2):
                 nc.scalar.activation(out=tanh_halves[h][t][:], in_=diff[t][:, h * HALF : (h + 1) * HALF], func=ACT.Tanh)
-        quantize(z_bf[:], z_codes[:], z_scales[:])
-
-        cv_win = tiles("cv_win", [P, WIDE], F32)
-        cv_plain = tiles("cv_plain", [P, N], F32)
-
-        def leave_bank(t, acc, lo, hi):
-            nc.scalar.activation(out=cv_win[t][:, lo:hi], in_=acc, func=ACT.Copy, scale=0.75 * 0.0625)
-            nc.scalar.activation(out=cv_plain[t][:, lo:hi], in_=acc, func=ACT.Copy, scale=0.0625)
 
         z2_codes = keep.tile([P, N], U32, name="z2_codes", align_bytes=64)
         z2_scales = keep.tile([P, N], U8, name="z2_scales", align_bytes=64)
@@ -197,27 +214,43 @@ def tile_picked_mombkindafdiflap_none_po_kernel(
             for t in range(PACK):
                 tanh = tanh_halves[lo // HALF][t][:, lo % HALF : lo % HALF + hi - lo]
                 nc.vector.tensor_tensor(z2[:, t, :], gb_win[t][:].indirect(entries(n5_sb, lo, hi)), tanh, ALU.mult)
-            interleave(nc.scalar.copy if hi < N else nc.vector.tensor_copy, z2_bf[:], z2)
-            quantize(z2_bf[:], z2_codes[:, lo:hi], z2_scales[:, lo:hi])
-            leave_bank(0, product(z_codes, z_scales, 0, z2_codes[:, lo:hi], z2_scales[:, lo:hi]), lo, hi)
+            interleave(nc.scalar.copy, z2_bf[:], z2)
+            return z2_bf
 
+        pieces = ((0, HALF), (HALF, HALF + QUARTER), (HALF + QUARTER, N))
         z2_low = keep.tile([P, PACK, HALF], F32, name="z2_low")
-        z2_columns(z2_low[:], 0, HALF)
-        z2_high = keep.tile([P, 2, PACK, QUARTER], F32, name="z2_high", tag="tanh_low3", align_bytes=64)
-        for c in range(2):
-            z2_columns(z2_high[:, c], HALF + c * QUARTER, HALF + (c + 1) * QUARTER)
+        quantize(z2_columns(z2_low[:], *pieces[0])[:], z2_codes[:, 0:HALF], z2_scales[:, 0:HALF])
+        z2_high = keep.tile([P, 2, PACK, QUARTER], F32, name="z2_high", tag="diff3", align_bytes=64)
+        z2_late = [z2_columns(z2_high[:, c], *pieces[1 + c]) for c in range(2)]
+
+        z_codes = keep.tile([P, H], U32, name="z_codes", tag="tanh_high2", align_bytes=64)
+        z_scales = keep.tile([P, H], U8, name="z_scales", align_bytes=64)
+        quantize(z_bf[:], z_codes[:], z_scales[:])
+        for z2_bf, (lo, hi) in zip(z2_late, pieces[1:]):
+            quantize(z2_bf[:], z2_codes[:, lo:hi], z2_scales[:, lo:hi])
+
+        cv_win = tiles("cv_win", [P, N], F32)
+        cv_plain = tiles("cv_plain", [P, N], F32)
+        first = [product(z_codes, z_scales, 0, z2_codes[:, lo:hi], z2_scales[:, lo:hi]) for lo, hi in pieces]
+        for acc, (lo, hi) in zip(first[:-1], pieces[:-1]):
+            nc.scalar.activation(out=cv_win[0][:, lo:hi], in_=acc, func=ACT.Copy, scale=WIN_SCALE)
+        nc.vector.tensor_scalar(cv_win[0][:, N - QUARTER : N], first[-1], WIN_SCALE, None, ALU.mult)
+        for acc, (lo, hi) in zip(first, pieces):
+            nc.scalar.activation(out=cv_plain[0][:, lo:hi], in_=acc, func=ACT.Copy, scale=CV_SCALE)
         for t in range(1, PACK):
-            leave_bank(t, product(z_codes, z_scales, t, z2_codes[:], z2_scales[:]), 0, N)
+            acc = product(z_codes, z_scales, t, z2_codes[:], z2_scales[:])
+            nc.scalar.activation(out=cv_win[t][:], in_=acc, func=ACT.Copy, scale=WIN_SCALE)
+            nc.scalar.activation(out=cv_plain[t][:], in_=acc, func=ACT.Copy, scale=CV_SCALE)
 
         out_rows = out_0.rearrange("(p t) c -> p t c", t=PACK)
         out_words = out_1[0].rearrange("p c r -> p (c r)").bitcast(I32)
         out_scales = keep.tile([P, N], U8, name="out_scales", align_bytes=64)
         part = tiles("part", [P, N], F32)
-        gate = keep.tile([P, HALF], F32, name="gate", tag="gate", align_bytes=64)
-        y_low = keep.tile([P, PACK, HALF], F32, name="y_low")
 
-        def y_rows(y, t, lo, other):
-            nc.vector.tensor_tensor(y[:, t, :], cv_win[t][:].indirect(entries(n7_sb, lo, lo + HALF)), other, ALU.add)
+        def y_rows(y, t, lo):
+            nc.vector.tensor_tensor(
+                y[:, t, :], cv_win[t][:].indirect(entries(n7_sb, lo, lo + HALF)), part[t][:, lo : lo + HALF], ALU.add
+            )
             nc.sync.dma_start(out_rows[:, t, lo : lo + HALF], y[:, t, :])
 
         def y_planes(y, lo, copies):
@@ -229,21 +262,20 @@ def tile_picked_mombkindafdiflap_none_po_kernel(
             quantize(y_bf[:], y_codes[:], out_scales[:, lo : lo + HALF])
             nc.sync.dma_start(out_words[:, lo : lo + HALF], y_codes[:].bitcast(I32))
 
-        last = PACK - 1
-        for t in range(last):
-            nc.vector.tensor_tensor(part[t][:], cv_win[t][:].indirect(n6_sb[:]), cv_plain[t][:], ALU.subtract)
-            y_rows(y_low, t, 0, part[t][:, 0:HALF])
-        nc.vector.tensor_tensor(
-            gate[:], cv_win[last][:].indirect(entries(n6_sb, 0, HALF)), cv_plain[last][:, 0:HALF], ALU.subtract
-        )
-        nc.vector.tensor_tensor(
-            part[last][:, HALF:N], cv_win[last][:].indirect(entries(n6_sb, HALF, N)), cv_plain[last][:, HALF:N], ALU.subtract
-        )
-        y_rows(y_low, last, 0, gate[:])
-        y_planes(y_low, 0, [nc.scalar.copy])
-        y_high = keep.tile([P, PACK, HALF], F32, name="y_high", tag="gate", align_bytes=64)
+        y_low = keep.tile([P, PACK, HALF], F32, name="y_low")
         for t in range(PACK):
-            y_rows(y_high, t, HALF, part[t][:, HALF:N])
+            for lo in (0, HALF):
+                nc.vector.tensor_tensor(
+                    part[t][:, lo : lo + HALF],
+                    cv_win[t][:].indirect(entries(n6_sb, lo, lo + HALF)),
+                    cv_plain[t][:, lo : lo + HALF],
+                    ALU.subtract,
+                )
+            y_rows(y_low, t, 0)
+        y_planes(y_low, 0, [nc.scalar.copy])
+        y_high = keep.tile([P, PACK, HALF], F32, name="y_high", tag="cv_plain3", align_bytes=64)
+        for t in range(PACK):
+            y_rows(y_high, t, HALF)
         y_planes(y_high, HALF, [nc.scalar.copy, nc.vector.tensor_copy])
         for q in range(4):
             queue = nc.scalar if q % 2 else nc.sync

@@ -214,7 +214,8 @@ def tile_picked_mombkindafdiflap_none_po_kernel(
             for t in range(PACK):
                 tanh = tanh_halves[lo // HALF][t][:, lo % HALF : lo % HALF + hi - lo]
                 nc.vector.tensor_tensor(z2[:, t, :], gb_win[t][:].indirect(entries(n5_sb, lo, hi)), tanh, ALU.mult)
-            interleave(nc.scalar.copy, z2_bf[:], z2)
+                if t % 2:
+                    interleave(nc.scalar.copy, z2_bf[:, :, t - 1 : t + 1], z2[:, t - 1 : t + 1, :])
             return z2_bf
 
         pieces = ((0, HALF), (HALF, HALF + QUARTER), (HALF + QUARTER, N))
@@ -256,9 +257,9 @@ def tile_picked_mombkindafdiflap_none_po_kernel(
         def y_planes(y, lo, copies):
             y_bf = keep.tile([P, HALF, PACK], BF16, name="y_bf16_%d" % lo, align_bytes=64)
             y_codes = keep.tile([P, HALF], U32, name="y_codes_%d" % lo, align_bytes=64)
-            share = HALF // len(copies)
+            share = PACK // len(copies)
             for c, copy in enumerate(copies):
-                interleave(copy, y_bf[:, c * share : (c + 1) * share, :], y[:, :, c * share : (c + 1) * share])
+                interleave(copy, y_bf[:, :, c * share : (c + 1) * share], y[:, c * share : (c + 1) * share, :])
             quantize(y_bf[:], y_codes[:], out_scales[:, lo : lo + HALF])
             nc.sync.dma_start(out_words[:, lo : lo + HALF], y_codes[:].bitcast(I32))
 

from contextlib import ExitStack

import concourse.mybir as mybir

K, T, S, N, H, J = 512, 2048, 512, 512, 512, 512
FLOPS = 2 * K * S * H + 2 * K * S * N + 2 * S * H * N

F32 = mybir.dt.float32
BF16 = mybir.dt.bfloat16
I32 = mybir.dt.int32
U32 = mybir.dt.uint32
U16 = mybir.dt.uint16
U8 = mybir.dt.uint8
FP8X4 = mybir.dt.float8_e4m3fn_x4
ALU = mybir.AluOpType
ACT = mybir.ActivationFunctionType

P = 128
PACK = 4
WIDE = 2 * 512
HALF = 256
QUARTER = 128
CV_SCALE = 0.0625
WIN_SCALE = 0.75 * CV_SCALE


def tile_picked_mombkindafdiflap_none_po_kernel(
    tc, x_words, x_scales, wa, wb, tab, gt, gi, offs, two, n1, n2, n3, n4, n5, n6, n7, out_0, out_1, out_2
):
    nc = tc.nc

    with ExitStack() as ctx:
        lists = ctx.enter_context(tc.tile_pool(name="lists", bufs=1))
        keep = ctx.enter_context(tc.tile_pool(name="keep", bufs=1))
        psum = ctx.enter_context(tc.psum_pool(name="psum", bufs=8))

        def load_list(name, src):
            held = lists.tile([P, S // 16], U16, name=name)
            nc.sync.dma_start(held[:], src)
            return held

        def entries(held, lo, hi):
            return held[:, lo // 16 : hi // 16]

        def tiles(name, shape, dtype):
            return [keep.tile(shape, dtype, name="%s%d" % (name, t), tag="%s%d" % (name, t), align_bytes=64) for t in range(PACK)]

        def mx_operand(name, width):
            rounded = keep.tile([P, width, PACK], BF16, name=name + "_bf16", tag=name + "_bf16", align_bytes=64)
            codes = keep.tile([P, width], U32, name=name + "_codes", align_bytes=64)
            scales = keep.tile([P, width], U8, name=name + "_scales", align_bytes=64)
            return rounded, codes, scales

        def quantize(rounded, codes, scales):
            nc.vector.quantize_mx(out=codes.bitcast(FP8X4), scales=scales, in_=rounded.rearrange("p c t -> p (c t)"))

        def interleave(copy, rounded, rows):
            copy(
                out=rounded.rearrange("p (c i) t -> p c t i", i=PACK),
                in_=rows.rearrange("p t (c i) -> p c t i", i=PACK),
            )

        def product(lhs_codes, lhs_scales, t, rhs_codes, rhs_scales):
            bank = psum.tile([P, 512], F32, name="bank")
            acc = bank[:, 0 : rhs_codes.shape[1]]
            cols = slice(t * P, (t + 1) * P)
            nc.tensor.matmul_mx(
                out=acc,
                lhsT=lhs_codes[:, cols].bitcast(FP8X4),
                lhsT_scale=lhs_scales[:, cols],
                rhs=rhs_codes.bitcast(FP8X4),
                rhs_scale=rhs_scales,
                start=True,
                stop=True,
            )
            return acc

        warm_in = keep.tile([P, 1], F32, name="warm_in")
        warm_out = keep.tile([P, 1], F32, name="warm_out")
        nc.gpsimd.memset(warm_in[:], 0.0)
        nc.scalar.activation(out=warm_out[:], in_=warm_in[:], func=ACT.Tanh)

        xs = keep.tile([P, T], U8, name="xs")
        nc.vector.memset(xs[:].bitcast(I32), 0)

        gt_sb = keep.tile([P, PACK], F32, name="gt_sb")
        gi_sb = keep.tile([P, PACK], F32, name="gi_sb")

        tab_rows = tab.rearrange("(p t) c -> p t c", t=PACK)
        tab_win = tiles("tab_win", [P, WIDE], F32)
        xw = keep.tile([P, T], U32, name="xw")

        def load_weights(name, w, h):
            raw = keep.tile([P, PACK, HALF], F32, name="%s_raw%d" % (name, h), tag="%s_raw%d" % (name, h), align_bytes=64)
            nc.sync.dma_start(raw[:], w.rearrange("(p j) c -> p j c", j=PACK)[:, :, h * HALF : (h + 1) * HALF])
            return raw

        nc.sync.dma_start(tab_win[0][:, 0:J], tab_rows[:, 0, :])
        n1_sb = load_list("n1_sb", n1)
        for t in range(1, PACK - 1):
            nc.sync.dma_start(tab_win[t][:, 0:J], tab_rows[:, t, :])
        nc.sync.dma_start(gt_sb[:], gt.rearrange("(p t) o -> p (t o)", t=PACK))
        nc.sync.dma_start(xw[:].bitcast(I32), x_words[0].rearrange("p c r -> p (c r)").bitcast(I32))
        offs_sb = load_list("offs_sb", offs)
        two_sb = load_list("two_sb", two)
        for q in range(4):
            nc.sync.dma_start(xs[32 * q : 32 * q + 4, :].bitcast(I32), x_scales[0][4 * q : 4 * q + 4, :].bitcast(I32))
        wa_raw = [load_weights("wa", wa, h) for h in range(2)]
        wb_raw = [load_weights("wb", wb, 0)]
        nc.sync.dma_start(tab_win[PACK - 1][:, 0:J], tab_rows[:, PACK - 1, :])
        n3_sb = load_list("n3_sb", n3)
        wb_raw.append(load_weights("wb", wb, 1))
        n2_sb = load_list("n2_sb", n2)
        nc.sync.dma_start(gi_sb[:], gi.rearrange("(p t) o -> p (t o)", t=PACK))
        n4_sb = load_list("n4_sb", n4)
        n5_sb = load_list("n5_sb", n5)
        n6_sb = load_list("n6_sb", n6)
        n7_sb = load_list("n7_sb", n7)

        last = PACK - 1
        tab_n1 = []

        def fetch_tab_n1(t, tag):
            tab_n1.append(keep.tile([P, H], F32, name="tab_n1_%d" % t, tag=tag, align_bytes=64))
            nc.vector.tensor_copy(tab_n1[t][:], tab_win[t][:].indirect(n1_sb[:]))

        def weigh_tab(t):
            nc.scalar.activation(out=tab_win[t][:, 0:J], in_=tab_win[t][:, 0:J], func=ACT.Copy, scale=gt_sb[:, t : t + 1])

        def pick(name, held):
            words = keep.tile([P, S], U32, name=name + "_words", align_bytes=64)
            picked = keep.tile([P, S], U8, name=name + "_picked", align_bytes=64)
            nc.vector.tensor_copy(words[:].rearrange("p (t m) -> p m t", t=PACK), xw[:].indirect(held[:]))
            nc.vector.tensor_copy(picked[:], xs[:].indirect(held[:]))
            return words, picked

        def deal(name, picked, tag):
            dealt = keep.tile([P, S], U8, name=name, tag=tag, align_bytes=64)
            nc.vector.tensor_copy(
                dealt[:].rearrange("p (t m) -> p t m", t=PACK), picked[:].rearrange("p (m t) -> p t m", t=PACK)
            )
            return dealt

        for t in range(last):
            fetch_tab_n1(t, "tab_n1_%d" % t)
            weigh_tab(t)
        xa_words, xa_picked = pick("xa", offs_sb)
        xb_words, xb_picked = pick("xb", two_sb)
        xa_scales = deal("xa_scales", xa_picked, "xa_scales")

        wa_bf, wa_codes, wa_scales = mx_operand("wa", H)
        for h in range(2):
            interleave(nc.scalar.copy, wa_bf[:, h * HALF : (h + 1) * HALF, :], wa_raw[h][:])
        quantize(wa_bf[:], wa_codes[:], wa_scales[:])
        xb_scales = deal("xb_scales", xb_picked, "wa_raw1")
        fetch_tab_n1(last, "wa_bf16")

        a_win = tiles("a_win", [P, WIDE], F32)
        for t in range(PACK):
            for lo, hi in ((0, HALF), (HALF, H)) if t == 0 else ((0, H),):
                acc = product(xa_words, xa_scales, t, wa_codes[:, lo:hi], wa_scales[:, lo:hi])
                nc.scalar.activation(out=a_win[t][:, lo:hi], in_=acc, func=ACT.Copy, scale=gt_sb[:, t : t + 1])

        wb_bf, wb_codes, wb_scales = mx_operand("wb", N)
        for h in range(2):
            interleave(nc.scalar.copy, wb_bf[:, h * HALF : (h + 1) * HALF, :], wb_raw[h][:])
        weigh_tab(last)

        a_tab = []

        def fetch_a(t, tag):
            a_tab.append(keep.tile([P, H], F32, name="a_tab%d" % t, tag=tag, align_bytes=64))
            nc.vector.tensor_tensor(a_tab[t][:], a_win[t][:].indirect(n3_sb[:]), tab_n1[t][:], ALU.mult)

        for t in range(last):
            fetch_a(t, "a_tab%d" % t)
        quantize(wb_bf[:], wb_codes[:], wb_scales[:])
        fetch_a(last, "wb_raw1")

        b_win = tiles("b_win", [P, WIDE], F32)
        b_plain = tiles("b_plain", [P, N], F32)
        gb_win = tiles("gb_win", [P, N], F32)
        b_acc = []
        for t in range(PACK):
            acc = product(xb_words, xb_scales, t, wb_codes[:], wb_scales[:])
            nc.scalar.copy(out=b_win[t][:, 0:N], in_=acc)
            nc.sync.dma_start(b_plain[t][:], b_win[t][:, 0:N])
            b_acc.append(acc)
        for t in range(PACK):
            nc.scalar.activation(out=gb_win[t][:], in_=b_acc[t], func=ACT.Copy, scale=gi_sb[:, t : t + 1])

        z = keep.tile([P, PACK, H], F32, name="z", tag="wb_bf16", align_bytes=64)
        for t in range(PACK):
            nc.vector.tensor_tensor(z[:, t, :], tab_win[t][:].indirect(n2_sb[:]), a_tab[t][:], ALU.add)

        z_bf = keep.tile([P, H, PACK], BF16, name="z_bf16", align_bytes=64)
        z_dealt = z_bf[:].rearrange("p (h m) t -> p m h t", h=PACK)
        z_quads = z[:].rearrange("p t (m h) -> p m h t", h=PACK)
        diff = tiles("diff", [P, N], F32)
        tanh_halves = (tiles("tanh_low", [P, HALF], F32), tiles("tanh_high", [P, HALF], F32))
        for t in range(PACK):
            nc.vector.tensor_tensor(diff[t][:], b_win[t][:].indirect(n4_sb[:]), b_plain[t][:], ALU.subtract)
            if t % 2 == 0:
                quads = slice(t * P // PACK, (t + 2) * P // PACK)
                nc.scalar.copy(out=z_dealt[:, quads], in_=z_quads[:, quads])
            for h in range(2):
                nc.scalar.activation(out=tanh_halves[h][t][:], in_=diff[t][:, h * HALF : (h + 1) * HALF], func=ACT.Tanh)

        z2_codes = keep.tile([P, N], U32, name="z2_codes", align_bytes=64)
        z2_scales = keep.tile([P, N], U8, name="z2_scales", align_bytes=64)

        def z2_columns(z2, lo, hi):
            z2_bf = keep.tile([P, hi - lo, PACK], BF16, name="z2_bf16_%d" % lo, align_bytes=64)
            for t in range(PACK):
                tanh = tanh_halves[lo // HALF][t][:, lo % HALF : lo % HALF + hi - lo]
                nc.vector.tensor_tensor(z2[:, t, :], gb_win[t][:].indirect(entries(n5_sb, lo, hi)), tanh, ALU.mult)
                if t % 2:
                    interleave(nc.scalar.copy, z2_bf[:, :, t - 1 : t + 1], z2[:, t - 1 : t + 1, :])
            return z2_bf

        pieces = ((0, HALF), (HALF, HALF + QUARTER), (HALF + QUARTER, N))
        z2_low = keep.tile([P, PACK, HALF], F32, name="z2_low")
        quantize(z2_columns(z2_low[:], *pieces[0])[:], z2_codes[:, 0:HALF], z2_scales[:, 0:HALF])
        z2_high = keep.tile([P, 2, PACK, QUARTER], F32, name="z2_high", tag="diff3", align_bytes=64)
        z2_late = [z2_columns(z2_high[:, c], *pieces[1 + c]) for c in range(2)]

        z_codes = keep.tile([P, H], U32, name="z_codes", tag="tanh_high2", align_bytes=64)
        z_scales = keep.tile([P, H], U8, name="z_scales", align_bytes=64)
        quantize(z_bf[:], z_codes[:], z_scales[:])
        for z2_bf, (lo, hi) in zip(z2_late, pieces[1:]):
            quantize(z2_bf[:], z2_codes[:, lo:hi], z2_scales[:, lo:hi])

        cv_win = tiles("cv_win", [P, N], F32)
        cv_plain = tiles("cv_plain", [P, N], F32)
        first = [product(z_codes, z_scales, 0, z2_codes[:, lo:hi], z2_scales[:, lo:hi]) for lo, hi in pieces]
        for acc, (lo, hi) in zip(first[:-1], pieces[:-1]):
            nc.scalar.activation(out=cv_win[0][:, lo:hi], in_=acc, func=ACT.Copy, scale=WIN_SCALE)
        nc.vector.tensor_scalar(cv_win[0][:, N - QUARTER : N], first[-1], WIN_SCALE, None, ALU.mult)
        for acc, (lo, hi) in zip(first, pieces):
            nc.scalar.activation(out=cv_plain[0][:, lo:hi], in_=acc, func=ACT.Copy, scale=CV_SCALE)
        for t in range(1, PACK):
            acc = product(z_codes, z_scales, t, z2_codes[:], z2_scales[:])
            nc.scalar.activation(out=cv_win[t][:], in_=acc, func=ACT.Copy, scale=WIN_SCALE)
            nc.scalar.activation(out=cv_plain[t][:], in_=acc, func=ACT.Copy, scale=CV_SCALE)

        out_rows = out_0.rearrange("(p t) c -> p t c", t=PACK)
        out_words = out_1[0].rearrange("p c r -> p (c r)").bitcast(I32)
        out_scales = keep.tile([P, N], U8, name="out_scales", align_bytes=64)
        part = tiles("part", [P, N], F32)

        def y_rows(y, t, lo):
            nc.vector.tensor_tensor(
                y[:, t, :], cv_win[t][:].indirect(entries(n7_sb, lo, lo + HALF)), part[t][:, lo : lo + HALF], ALU.add
            )
            nc.sync.dma_start(out_rows[:, t, lo : lo + HALF], y[:, t, :])

        def y_planes(y, lo, copies):
            y_bf = keep.tile([P, HALF, PACK], BF16, name="y_bf16_%d" % lo, align_bytes=64)
            y_codes = keep.tile([P, HALF], U32, name="y_codes_%d" % lo, align_bytes=64)
            share = PACK // len(copies)
            for c, copy in enumerate(copies):
                interleave(copy, y_bf[:, :, c * share : (c + 1) * share], y[:, c * share : (c + 1) * share, :])
            quantize(y_bf[:], y_codes[:], out_scales[:, lo : lo + HALF])
            nc.sync.dma_start(out_words[:, lo : lo + HALF], y_codes[:].bitcast(I32))

        y_low = keep.tile([P, PACK, HALF], F32, name="y_low")
        for t in range(PACK):
            for lo in (0, HALF):
                nc.vector.tensor_tensor(
                    part[t][:, lo : lo + HALF],
                    cv_win[t][:].indirect(entries(n6_sb, lo, lo + HALF)),
                    cv_plain[t][:, lo : lo + HALF],
                    ALU.subtract,
                )
            y_rows(y_low, t, 0)
        y_planes(y_low, 0, [nc.scalar.copy])
        y_high = keep.tile([P, PACK, HALF], F32, name="y_high", tag="cv_plain3", align_bytes=64)
        for t in range(PACK):
            y_rows(y_high, t, HALF)
        y_planes(y_high, HALF, [nc.scalar.copy, nc.vector.tensor_copy])
        for q in range(4):
            queue = nc.scalar if q % 2 else nc.sync
            queue.dma_start(
                out_2[0][4 * q : 4 * q + 4, :].bitcast(I32), out_scales[32 * q : 32 * q + 4, :].bitcast(I32)
            )
